import numpy as np
import ml_dtypes


def mxq(x, axis, fmt="e4m3"):
    dtype, down = {"e4m3": (ml_dtypes.float8_e4m3fn, 7), "e5m2": (ml_dtypes.float8_e5m2, 14)}[fmt]
    v = np.moveaxis(np.asarray(x, np.float32).astype(ml_dtypes.bfloat16).astype(np.float64), axis, -1)
    blocks = v.reshape(v.shape[:-1] + (-1, 32))
    amax = np.abs(blocks).max(-1, keepdims=True)
    byte = np.maximum(np.where(amax > 0, np.frexp(amax)[1] - 1 + 127, 0) - down, 1)
    scale = np.exp2(byte - 127.0)
    codes = (blocks / scale).astype(np.float32).astype(dtype).astype(np.float64)
    return np.moveaxis((codes * scale).reshape(v.shape), -1, axis)


WIDE = False


def mx_kscale(k):
    if not WIDE:
        return np.ones(k)
    levels = np.array([10, -10, 5, -5, 0])
    if k % 512:
        return np.exp2(np.random.permutation(np.resize(levels, k // 32))).repeat(32)
    a = np.empty((k // 512, 16))
    for p in range(k // 512):
        a[p, :8] = np.random.permutation(np.resize(levels, 8))
        for g in range(8):
            far = levels[np.abs(levels - a[p, g]) >= 10]
            a[p, g + 8] = far[np.random.randint(len(far))]
    return np.exp2(a.ravel()).repeat(32)


def f64(x):
    return np.asarray(x).astype(np.float64)


def striped(idx):
    return np.tile(np.asarray(idx).reshape(-1, 16).T, (8, 1)).astype(np.uint16)


def unstriped(offs):
    return offs[:16].T.reshape(-1).astype(np.int64)


E2M1 = np.array([0.0, 0.5, 1.0, 1.5, 2.0, 3.0, 4.0, 6.0, -0.0, -0.5, -1.0, -1.5, -2.0, -3.0, -4.0, -6.0])


def pack_weight(w, fmt):
    k, n = w.shape
    w = f64(np.asarray(w, np.float32).astype(ml_dtypes.bfloat16)).reshape(k // 32, 32, n)
    amax = np.abs(w).max(1)
    if fmt == "e4m3":
        byte = np.frexp(amax)[1] - 1 + 127 - 7
    else:
        mant, ex = np.frexp(amax / 6.0)
        byte = np.where(mant > 0.5, ex, ex - 1) + 127
    byte = np.clip(np.where(amax > 0, byte, 1), 1, 254)
    scaled = (w * np.exp2(127.0 - byte)[:, None, :]).reshape(k, n).astype(np.float32)
    by_word = np.ascontiguousarray(scaled.reshape(k // 512, 128, 4, n).transpose(0, 1, 3, 2))
    if fmt == "e4m3":
        words = by_word.astype(ml_dtypes.float8_e4m3fn).view(np.uint8)
    else:
        c = by_word.astype(ml_dtypes.float4_e2m1fn).view(np.uint8) & 0xF
        words = (c[..., 0::2] | (c[..., 1::2] << 4)).reshape(k // 512, 128, 2 * n)
    return np.ascontiguousarray(words), np.ascontiguousarray(byte.astype(np.uint8).reshape(k // 512, 16, n))


def unpack_weight(words, scales, fmt):
    g, _, n = scales.shape
    words = np.ascontiguousarray(words).reshape(g, 128, n, -1)
    if fmt == "e4m3":
        vals = words.view(ml_dtypes.float8_e4m3fn).astype(np.float64)
    else:
        nib = np.empty((g, 128, n, 4), np.uint8)
        nib[..., 0::2] = words & 0xF
        nib[..., 1::2] = words >> 4
        vals = E2M1[nib]
    vals = vals * np.repeat(np.exp2(scales.astype(np.float64) - 127.0), 8, axis=1)[..., None]
    return vals.transpose(0, 1, 3, 2).reshape(g * 512, n)


def bf(x):
    return np.asarray(x, np.float32).astype(ml_dtypes.bfloat16)


def planes(Y):
    r, m = Y.shape
    b = f64(bf(Y)).reshape(r // 32, 32, m)
    amax = np.abs(b).max(1)
    byte = np.clip(np.where(amax > 0, np.frexp(amax)[1] - 1 + 127 - 7, 1), 1, 254)
    codes = (b * np.exp2(127.0 - byte)[:, None, :]).reshape(r, m).astype(np.float32).astype(ml_dtypes.float8_e4m3fn).view(np.uint8)
    words = codes.reshape(r // 512, 128, 4, m).transpose(0, 1, 3, 2)
    return np.ascontiguousarray(words), np.ascontiguousarray(byte.astype(np.uint8).reshape(r // 512, 16, m))


K, T, J, R, V, N = 512, 2048, 512, 512, 1024, 512


def setup_inputs():
    n = np.random.standard_normal
    idx = np.random.permutation(T)[:J]
    idx2 = np.random.permutation(V)[:J]
    fk = mx_kscale(K)
    fr = mx_kscale(R)
    xtp = pack_weight(n((K, T)) / fk[:, None], "e2m1")
    wap = pack_weight(n((K, R)) * 1 / np.sqrt(K) * fk[:, None] * fr, "e4m3")
    wbp = pack_weight(n((R, N)) * 1 / np.sqrt(R) / fr[:, None], "e2m1")
    return {
        "xt_words": xtp[0],
        "xt_scales": xtp[1],
        "wa_words": wap[0],
        "wa_scales": wap[1],
        "tb": (n((R, V)) * fr[:, None]).astype(np.float32),
        "wb_words": wbp[0],
        "wb_scales": wbp[1],
        "rw": (np.random.uniform(0.5, 2.0, (1, J))).astype(np.float32),
        "offs": striped(idx),
        "offs2": striped(idx2),
    }


def reference(xt_words, xt_scales, wa_words, wa_scales, tb, wb_words, wb_scales, rw, offs, offs2):
    idx = unstriped(offs)
    idx2 = unstriped(offs2)
    xtu = unpack_weight(xt_words, xt_scales, "e2m1")
    wau = unpack_weight(wa_words, wa_scales, "e4m3")
    wbu = unpack_weight(wb_words, wb_scales, "e2m1")
    xtidxg = xtu[:, idx]
    a = wau.T @ xtidxg
    hid = np.maximum(a, f64(tb)[:, idx2])
    hidq = mxq(hid, 0, "e4m3")
    p = wbu.T @ hidq
    y = p * f64(rw)
    words, scales = planes(y)
    return y, words, scales

@@ -1,0 +1,231 @@
+from contextlib import ExitStack
+
+import concourse.mybir as mybir
+from concourse.masks import make_identity
+
+K, T, J, R, V, N = 512, 2048, 512, 512, 1024, 512
+FLOPS = 2 * K * R * J + 2 * R * N * J
+
+F32 = mybir.dt.float32
+BF16 = mybir.dt.bfloat16
+I32 = mybir.dt.int32
+U32 = mybir.dt.uint32
+U16 = mybir.dt.uint16
+U8 = mybir.dt.uint8
+FP8X4 = mybir.dt.float8_e4m3fn_x4
+FP4X4 = mybir.dt.float4_e2m1fn_x4
+COPY = mybir.ActivationFunctionType.Copy
+MAX = mybir.AluOpType.max
+
+P = 128
+PACK = 4
+CHUNK = 128
+CHUNKS = J // CHUNK
+LIST_COLS = CHUNK // 16
+TURNED = 2
+MULT = mybir.AluOpType.mult
+
+
+def load_scales(queue, plane, rows):
+    for q in range(4):
+        queue.dma_start(out=plane[32 * q : 32 * q + 4, :].bitcast(I32), in_=rows[4 * q : 4 * q + 4, :].bitcast(I32))
+
+
+def by_lines(planes):
+    return planes.rearrange("p t (c i) -> p c t i", i=PACK)
+
+
+def woven(tile):
+    return tile.rearrange("p (c i t) -> p c t i", i=PACK, t=PACK)
+
+
+def tile_list_hidden_above_table_pl_kernel(
+    tc, xt_words, xt_scales, wa_words, wa_scales, tb, wb_words, wb_scales, rw, offs, offs2, out_0, out_1, out_2
+):
+    nc = tc.nc
+    with ExitStack() as ctx:
+        keep = ctx.enter_context(tc.tile_pool(name="keep", bufs=1))
+        psum = ctx.enter_context(tc.psum_pool(name="psum", bufs=1))
+
+        def bank(b):
+            return psum.tile([P, 512], F32, name="bank%d" % b, tag="bank%d" % b)
+
+        idx = keep.tile([P, J // 16], U16, name="idx")
+        idx2 = keep.tile([P, J // 16], U16, name="idx2")
+        xw = keep.tile([P, T], U16, name="xw", align_bytes=64)
+        xs = keep.tile([P, T], U8, name="xs", align_bytes=64)
+        waw = keep.tile([P, R], U32, name="waw", align_bytes=64)
+        was = keep.tile([P, R], U8, name="was", align_bytes=64)
+        wbw = keep.tile([P, N], U16, name="wbw", align_bytes=64)
+        wbs = keep.tile([P, N], U8, name="wbs", align_bytes=64)
+        rwc = keep.tile([P, CHUNKS], F32, name="rwc")
+        ident = keep.tile([P, P], F32, name="ident")
+        table = [keep.tile([P, V], F32, name="table%d" % t) for t in range(PACK)]
+
+        nc.gpsimd.memset(xs[:].bitcast(I32), 0)
+        nc.vector.memset(was[:].bitcast(I32), 0)
+        nc.vector.memset(wbs[:].bitcast(I32), 0)
+        make_identity(nc, ident[:])
+
+        tb_rows = tb.rearrange("(p t) v -> p t v", t=PACK)
+        nc.sync.dma_start(idx[:], offs)
+        nc.sync.dma_start(out=xw[:].bitcast(I32), in_=xt_words[0].bitcast(I32))
+        nc.sync.dma_start(idx2[:], offs2)
+        nc.sync.dma_start(out=table[0][:], in_=tb_rows[:, 0, :])
+        load_scales(nc.sync, xs, xt_scales[0])
+        nc.sync.dma_start(out=waw[:].bitcast(I32), in_=wa_words[0].rearrange("p c r -> p (c r)").bitcast(I32))
+        nc.sync.dma_start(out=table[1][:], in_=tb_rows[:, 1, :])
+        load_scales(nc.sync, was, wa_scales[0])
+        for t in range(2, PACK):
+            nc.sync.dma_start(out=table[t][:], in_=tb_rows[:, t, :])
+        nc.sync.dma_start(out=wbw[:].bitcast(I32), in_=wb_words[0].bitcast(I32))
+        load_scales(nc.sync, wbs, wb_scales[0])
+        with nc.allow_non_contiguous_dma(reason="one slot weight a partition and chunk"):
+            nc.sync.dma_start(out=rwc[:], in_=rw[0].rearrange("(c p) -> p c", p=P))
+
+        xg = keep.tile([P, J], U16, name="xg", align_bytes=64)
+        xsg = keep.tile([P, J], U8, name="xsg", align_bytes=64)
+        floor = keep.tile([P, PACK * J], F32, name="floor")
+        floor_planes = floor[:].rearrange("p (t j) -> p t j", t=PACK)
+
+        nc.vector.tensor_copy(xg[:], xw[:].indirect(idx[:]))
+        nc.vector.tensor_copy(floor[:, 0:J], table[0][:].indirect(idx2[:]))
+        nc.vector.tensor_copy(xsg[:], xs[:].indirect(idx[:]))
+        for t in range(1, PACK - 1):
+            nc.vector.tensor_copy(floor[:, t * J : (t + 1) * J], table[t][:].indirect(idx2[:]))
+
+        wbw_dealt = keep.tile([P, N], U16, name="wbw_dealt", align_bytes=64)
+        wbs_dealt = keep.tile([P, N], U8, name="wbs_dealt", align_bytes=64)
+        nc.vector.tensor_copy(
+            out=wbw_dealt[:].rearrange("p (t c i) -> p c t i", t=PACK, i=8),
+            in_=wbw[:].rearrange("p (c i t) -> p c t i", t=PACK, i=8),
+        )
+        nc.vector.tensor_copy(
+            out=wbs_dealt[:].rearrange("p (t c i) -> p c t i", t=PACK, i=16),
+            in_=wbs[:].rearrange("p (c i t) -> p c t i", t=PACK, i=16),
+        )
+
+        def turn(rows, dst):
+            for t in range(PACK):
+                nc.tensor.transpose(dst[:, t * P : (t + 1) * P], rows[:, t * P : (t + 1) * P], ident[:])
+
+        a_banks = []
+        for c in range(CHUNKS):
+            cols = slice(c * CHUNK, (c + 1) * CHUNK)
+            a_t = bank(CHUNKS + c)
+            nc.tensor.matmul_mx(
+                out=a_t[:],
+                lhsT=xg[:, cols].bitcast(FP4X4),
+                lhsT_scale=xsg[:, cols],
+                rhs=waw[:].bitcast(FP8X4),
+                rhs_scale=was[:],
+                start=True,
+                stop=True,
+            )
+            a_rows = keep.tile([P, R], F32, name="a_rows%d" % c)
+            nc.scalar.copy(
+                out=a_rows[:].rearrange("p (t m) -> p t m", t=PACK),
+                in_=a_t[:].rearrange("p (m t) -> p t m", t=PACK),
+            )
+            a_bank = bank(c)
+            turn(a_rows, a_bank)
+            a_banks.append(a_bank)
+
+        last = PACK - 1
+        hid_codes = []
+        hid_scales = []
+        for c in range(CHUNKS):
+            cols = slice(c * CHUNK, (c + 1) * CHUNK)
+            nc.vector.tensor_copy(
+                floor[:, last * J + c * CHUNK : last * J + (c + 1) * CHUNK],
+                table[last][:].indirect(idx2[:, c * LIST_COLS : (c + 1) * LIST_COLS]),
+            )
+            hid = keep.tile([P, PACK * CHUNK], BF16, name="hid%d" % c, align_bytes=64)
+            nc.vector.tensor_tensor(
+                out=woven(hid[:]),
+                in0=by_lines(a_banks[c][:].rearrange("p (t j) -> p t j", t=PACK)),
+                in1=by_lines(floor_planes[:, :, cols]),
+                op=MAX,
+            )
+            codes = keep.tile([P, CHUNK], U32, name="hid_codes%d" % c, align_bytes=64)
+            scales = keep.tile([P, CHUNK], U8, name="hid_scales%d" % c, align_bytes=64)
+            nc.vector.quantize_mx(out=codes[:].bitcast(FP8X4), scales=scales[:], in_=hid[:])
+            hid_codes.append(codes)
+            hid_scales.append(scales)
+
+        y_codes = keep.tile([P, J], U32, name="y_codes", align_bytes=64)
+        y_scales = keep.tile([P, J], U8, name="y_scales", align_bytes=64)
+        out_rows = out_0.rearrange("(p t) j -> p t j", t=PACK)
+        out_words = out_1[0].rearrange("p c r -> p (c r)").bitcast(I32)
+        ys = [keep.tile([P, PACK * CHUNK], F32, name="y%d" % c) for c in range(CHUNKS)]
+        y_planes = [y[:].rearrange("p (t j) -> p t j", t=PACK) for y in ys]
+        y_bf = [keep.tile([P, PACK * CHUNK], BF16, name="y_bf%d" % c, align_bytes=64) for c in range(CHUNKS)]
+
+        spread = CHUNKS - TURNED
+        rw_bank = bank(2 * CHUNKS - 1)
+        for s in range(spread):
+            c = TURNED + s
+            nc.tensor.transpose(rw_bank[:, s * P : (s + 1) * P], rwc[:, c : c + 1].to_broadcast([P, P]), ident[:])
+        rw_rows = keep.tile([P, spread * CHUNK], F32, name="rw_rows")
+        nc.scalar.copy(out=rw_rows[:], in_=rw_bank[:, : spread * P])
+
+        for c in range(TURNED):
+            cols = slice(c * CHUNK, (c + 1) * CHUNK)
+            p_t = bank(CHUNKS + c)
+            nc.tensor.matmul_mx(
+                out=p_t[:],
+                lhsT=hid_codes[c][:].bitcast(FP8X4),
+                lhsT_scale=hid_scales[c][:],
+                rhs=wbw[:].bitcast(FP4X4),
+                rhs_scale=wbs[:],
+                start=True,
+                stop=True,
+            )
+            y_rows = keep.tile([P, N], F32, name="y_rows%d" % c)
+            nc.scalar.activation(
+                out=y_rows[:].rearrange("p (t m) -> p t m", t=PACK),
+                in_=p_t[:].rearrange("p (m t) -> p t m", t=PACK),
+                func=COPY,
+                scale=rwc[:, c : c + 1],
+            )
+            y_bank = bank(c)
+            turn(y_rows, y_bank)
+            nc.scalar.copy(out=ys[c][:], in_=y_bank[:])
+            nc.sync.dma_start(out=out_rows[:, :, cols], in_=y_planes[c])
+
+        for c in range(TURNED, CHUNKS):
+            cols = slice(c * CHUNK, (c + 1) * CHUNK)
+            p_bank = bank(CHUNKS + c)
+            for t in range(PACK):
+                nc.tensor.matmul_mx(
+                    out=p_bank[:, t * CHUNK : (t + 1) * CHUNK],
+                    lhsT=wbw_dealt[:, t * P : (t + 1) * P].bitcast(FP4X4),
+                    lhsT_scale=wbs_dealt[:, t * P : (t + 1) * P],
+                    rhs=hid_codes[c][:].bitcast(FP8X4),
+                    rhs_scale=hid_scales[c][:],
+                    start=True,
+                    stop=True,
+                )
+            s = c - TURNED
+            nc.vector.tensor_tensor(
+                out=y_planes[c],
+                in0=p_bank[:].rearrange("p (t j) -> p t j", t=PACK),
+                in1=rw_rows[:, s * CHUNK : (s + 1) * CHUNK].unsqueeze(1).to_broadcast([P, PACK, CHUNK]),
+                op=MULT,
+            )
+            nc.sync.dma_start(out=out_rows[:, :, cols], in_=y_planes[c])
+            nc.scalar.copy(out=woven(y_bf[c][:]), in_=by_lines(y_planes[c]))
+
+        for c in range(CHUNKS):
+            cols = slice(c * CHUNK, (c + 1) * CHUNK)
+            if c < TURNED:
+                nc.vector.tensor_copy(out=woven(y_bf[c][:]), in_=by_lines(y_planes[c]))
+            nc.vector.quantize_mx(out=y_codes[:, cols].bitcast(FP8X4), scales=y_scales[:, cols], in_=y_bf[c][:])
+            if c == CHUNKS - 2:
+                nc.sync.dma_start(out=out_words[:, : (c + 1) * CHUNK], in_=y_codes[:, : (c + 1) * CHUNK].bitcast(I32))
+        nc.sync.dma_start(out=out_words[:, last * CHUNK :], in_=y_codes[:, last * CHUNK :].bitcast(I32))
+        for q in range(4):
+            queue = nc.scalar if q % 2 else nc.sync
+            queue.dma_start(
+                out=out_2[0, 4 * q : 4 * q + 4, :].bitcast(I32), in_=y_scales[32 * q : 32 * q + 4, :].bitcast(I32)
+            )

@@ -22,7 +22,7 @@ PACK = 4
 CHUNK = 128
 CHUNKS = J // CHUNK
 LIST_COLS = CHUNK // 16
-TURNED = 2
+TURNED = 0
 MULT = mybir.AluOpType.mult
 
 
@@ -56,28 +56,27 @@ def tile_list_hidden_above_table_pl_kernel(
         xs = keep.tile([P, T], U8, name="xs", align_bytes=64)
         waw = keep.tile([P, R], U32, name="waw", align_bytes=64)
         was = keep.tile([P, R], U8, name="was", align_bytes=64)
-        wbw = keep.tile([P, N], U16, name="wbw", align_bytes=64)
-        wbs = keep.tile([P, N], U8, name="wbs", align_bytes=64)
+        wbw = keep.tile([P, N], U16, name="wbw", tag="hid1", align_bytes=64)
+        wbs = keep.tile([P, N], U8, name="wbs", tag="hid2", align_bytes=64)
         rwc = keep.tile([P, CHUNKS], F32, name="rwc")
         ident = keep.tile([P, P], F32, name="ident")
         table = [keep.tile([P, V], F32, name="table%d" % t) for t in range(PACK)]
 
-        nc.gpsimd.memset(xs[:].bitcast(I32), 0)
-        nc.vector.memset(was[:].bitcast(I32), 0)
+        nc.vector.memset(xs[:].bitcast(I32), 0)
+        nc.gpsimd.memset(was[:].bitcast(I32), 0)
         nc.vector.memset(wbs[:].bitcast(I32), 0)
         make_identity(nc, ident[:])
 
         tb_rows = tb.rearrange("(p t) v -> p t v", t=PACK)
         nc.sync.dma_start(idx[:], offs)
         nc.sync.dma_start(out=xw[:].bitcast(I32), in_=xt_words[0].bitcast(I32))
-        nc.sync.dma_start(idx2[:], offs2)
-        nc.sync.dma_start(out=table[0][:], in_=tb_rows[:, 0, :])
         load_scales(nc.sync, xs, xt_scales[0])
         nc.sync.dma_start(out=waw[:].bitcast(I32), in_=wa_words[0].rearrange("p c r -> p (c r)").bitcast(I32))
-        nc.sync.dma_start(out=table[1][:], in_=tb_rows[:, 1, :])
-        load_scales(nc.sync, was, wa_scales[0])
-        for t in range(2, PACK):
+        nc.sync.dma_start(idx2[:], offs2)
+        for t in range(PACK):
             nc.sync.dma_start(out=table[t][:], in_=tb_rows[:, t, :])
+            if t == 1:
+                load_scales(nc.sync, was, wa_scales[0])
         nc.sync.dma_start(out=wbw[:].bitcast(I32), in_=wb_words[0].bitcast(I32))
         load_scales(nc.sync, wbs, wb_scales[0])
         with nc.allow_non_contiguous_dma(reason="one slot weight a partition and chunk"):
@@ -89,21 +88,9 @@ def tile_list_hidden_above_table_pl_kernel(
         floor_planes = floor[:].rearrange("p (t j) -> p t j", t=PACK)
 
         nc.vector.tensor_copy(xg[:], xw[:].indirect(idx[:]))
-        nc.vector.tensor_copy(floor[:, 0:J], table[0][:].indirect(idx2[:]))
         nc.vector.tensor_copy(xsg[:], xs[:].indirect(idx[:]))
-        for t in range(1, PACK - 1):
+        for t in range(PACK - 1):
             nc.vector.tensor_copy(floor[:, t * J : (t + 1) * J], table[t][:].indirect(idx2[:]))
-
-        wbw_dealt = keep.tile([P, N], U16, name="wbw_dealt", align_bytes=64)
-        wbs_dealt = keep.tile([P, N], U8, name="wbs_dealt", align_bytes=64)
-        nc.vector.tensor_copy(
-            out=wbw_dealt[:].rearrange("p (t c i) -> p c t i", t=PACK, i=8),
-            in_=wbw[:].rearrange("p (c i t) -> p c t i", t=PACK, i=8),
-        )
-        nc.vector.tensor_copy(
-            out=wbs_dealt[:].rearrange("p (t c i) -> p c t i", t=PACK, i=16),
-            in_=wbs[:].rearrange("p (c i t) -> p c t i", t=PACK, i=16),
-        )
 
         def turn(rows, dst):
             for t in range(PACK):
@@ -131,6 +118,8 @@ def tile_list_hidden_above_table_pl_kernel(
             turn(a_rows, a_bank)
             a_banks.append(a_bank)
 
+        wbw_dealt = keep.tile([P, N], U16, name="wbw_dealt", align_bytes=64)
+        wbs_dealt = keep.tile([P, N], U8, name="wbs_dealt", align_bytes=64)
         last = PACK - 1
         hid_codes = []
         hid_scales = []
@@ -140,18 +129,32 @@ def tile_list_hidden_above_table_pl_kernel(
                 floor[:, last * J + c * CHUNK : last * J + (c + 1) * CHUNK],
                 table[last][:].indirect(idx2[:, c * LIST_COLS : (c + 1) * LIST_COLS]),
             )
-            hid = keep.tile([P, PACK * CHUNK], BF16, name="hid%d" % c, align_bytes=64)
+            if c < 2:
+                hid = keep.tile([P, PACK * CHUNK], BF16, name="hid%d" % c, tag="hid%d" % c, align_bytes=64)[:]
+            else:
+                if c == 2:
+                    hid_late = keep.tile([P, 2 * PACK * CHUNK], BF16, name="hid_late", tag="hid2", align_bytes=64)
+                hid = hid_late[:, (c - 2) * PACK * CHUNK : (c - 1) * PACK * CHUNK]
             nc.vector.tensor_tensor(
-                out=woven(hid[:]),
+                out=woven(hid),
                 in0=by_lines(a_banks[c][:].rearrange("p (t j) -> p t j", t=PACK)),
                 in1=by_lines(floor_planes[:, :, cols]),
                 op=MAX,
             )
             codes = keep.tile([P, CHUNK], U32, name="hid_codes%d" % c, align_bytes=64)
             scales = keep.tile([P, CHUNK], U8, name="hid_scales%d" % c, align_bytes=64)
-            nc.vector.quantize_mx(out=codes[:].bitcast(FP8X4), scales=scales[:], in_=hid[:])
+            nc.vector.quantize_mx(out=codes[:].bitcast(FP8X4), scales=scales[:], in_=hid)
             hid_codes.append(codes)
             hid_scales.append(scales)
+            if c == 0:
+                nc.vector.tensor_copy(
+                    out=wbw_dealt[:].rearrange("p (t c i) -> p c t i", t=PACK, i=8),
+                    in_=wbw[:].rearrange("p (c i t) -> p c t i", t=PACK, i=8),
+                )
+                nc.vector.tensor_copy(
+                    out=wbs_dealt[:].rearrange("p (t c i) -> p c t i", t=PACK, i=16),
+                    in_=wbs[:].rearrange("p (c i t) -> p c t i", t=PACK, i=16),
+                )
 
         y_codes = keep.tile([P, J], U32, name="y_codes", align_bytes=64)
         y_scales = keep.tile([P, J], U8, name="y_scales", align_bytes=64)
@@ -207,14 +210,23 @@ def tile_list_hidden_above_table_pl_kernel(
                     stop=True,
                 )
             s = c - TURNED
-            nc.vector.tensor_tensor(
-                out=y_planes[c],
-                in0=p_bank[:].rearrange("p (t j) -> p t j", t=PACK),
-                in1=rw_rows[:, s * CHUNK : (s + 1) * CHUNK].unsqueeze(1).to_broadcast([P, PACK, CHUNK]),
-                op=MULT,
-            )
+            parts = 2 if c == CHUNKS - 1 else 1
+            width = CHUNK // parts
+            for h in range(parts):
+                part = slice(h * width, (h + 1) * width)
+                nc.vector.tensor_tensor(
+                    out=y_planes[c][:, :, part],
+                    in0=p_bank[:].rearrange("p (t j) -> p t j", t=PACK)[:, :, part],
+                    in1=rw_rows[:, s * CHUNK + h * width : s * CHUNK + (h + 1) * width]
+                    .unsqueeze(1)
+                    .to_broadcast([P, PACK, width]),
+                    op=MULT,
+                )
+                nc.scalar.copy(
+                    out=woven(y_bf[c][:, PACK * h * width : PACK * (h + 1) * width]),
+                    in_=by_lines(y_planes[c][:, :, part]),
+                )
             nc.sync.dma_start(out=out_rows[:, :, cols], in_=y_planes[c])
-            nc.scalar.copy(out=woven(y_bf[c][:]), in_=by_lines(y_planes[c]))
 
         for c in range(CHUNKS):
             cols = slice(c * CHUNK, (c + 1) * CHUNK)

@@ -56,8 +56,8 @@ def tile_list_hidden_above_table_pl_kernel(
         xs = keep.tile([P, T], U8, name="xs", align_bytes=64)
         waw = keep.tile([P, R], U32, name="waw", align_bytes=64)
         was = keep.tile([P, R], U8, name="was", align_bytes=64)
-        wbw = keep.tile([P, N], U16, name="wbw", tag="hid1", align_bytes=64)
-        wbs = keep.tile([P, N], U8, name="wbs", tag="hid2", align_bytes=64)
+        wbw = keep.tile([P, N], U16, name="wbw", tag="hid0", align_bytes=64)
+        wbs = keep.tile([P, N], U8, name="wbs", tag="hid1", align_bytes=64)
         rwc = keep.tile([P, CHUNKS], F32, name="rwc")
         ident = keep.tile([P, P], F32, name="ident")
         table = [keep.tile([P, V], F32, name="table%d" % t) for t in range(PACK)]
@@ -121,6 +121,14 @@ def tile_list_hidden_above_table_pl_kernel(
         wbw_dealt = keep.tile([P, N], U16, name="wbw_dealt", align_bytes=64)
         wbs_dealt = keep.tile([P, N], U8, name="wbs_dealt", align_bytes=64)
         last = PACK - 1
+        nc.vector.tensor_copy(
+            out=wbw_dealt[:].rearrange("p (t c i) -> p c t i", t=PACK, i=8),
+            in_=wbw[:].rearrange("p (c i t) -> p c t i", t=PACK, i=8),
+        )
+        nc.vector.tensor_copy(
+            out=wbs_dealt[:].rearrange("p (t c i) -> p c t i", t=PACK, i=16),
+            in_=wbs[:].rearrange("p (c i t) -> p c t i", t=PACK, i=16),
+        )
         hid_codes = []
         hid_scales = []
         for c in range(CHUNKS):
@@ -129,12 +137,12 @@ def tile_list_hidden_above_table_pl_kernel(
                 floor[:, last * J + c * CHUNK : last * J + (c + 1) * CHUNK],
                 table[last][:].indirect(idx2[:, c * LIST_COLS : (c + 1) * LIST_COLS]),
             )
-            if c < 2:
+            if c < 1:
                 hid = keep.tile([P, PACK * CHUNK], BF16, name="hid%d" % c, tag="hid%d" % c, align_bytes=64)[:]
             else:
-                if c == 2:
-                    hid_late = keep.tile([P, 2 * PACK * CHUNK], BF16, name="hid_late", tag="hid2", align_bytes=64)
-                hid = hid_late[:, (c - 2) * PACK * CHUNK : (c - 1) * PACK * CHUNK]
+                if c == 1:
+                    hid_late = keep.tile([P, 3 * PACK * CHUNK], BF16, name="hid_late", tag="hid1", align_bytes=64)
+                hid = hid_late[:, (c - 1) * PACK * CHUNK : c * PACK * CHUNK]
             nc.vector.tensor_tensor(
                 out=woven(hid),
                 in0=by_lines(a_banks[c][:].rearrange("p (t j) -> p t j", t=PACK)),
@@ -146,22 +154,15 @@ def tile_list_hidden_above_table_pl_kernel(
             nc.vector.quantize_mx(out=codes[:].bitcast(FP8X4), scales=scales[:], in_=hid)
             hid_codes.append(codes)
             hid_scales.append(scales)
-            if c == 0:
-                nc.vector.tensor_copy(
-                    out=wbw_dealt[:].rearrange("p (t c i) -> p c t i", t=PACK, i=8),
-                    in_=wbw[:].rearrange("p (c i t) -> p c t i", t=PACK, i=8),
-                )
-                nc.vector.tensor_copy(
-                    out=wbs_dealt[:].rearrange("p (t c i) -> p c t i", t=PACK, i=16),
-                    in_=wbs[:].rearrange("p (c i t) -> p c t i", t=PACK, i=16),
-                )
 
-        y_codes = keep.tile([P, J], U32, name="y_codes", align_bytes=64)
         y_scales = keep.tile([P, J], U8, name="y_scales", align_bytes=64)
         out_rows = out_0.rearrange("(p t) j -> p t j", t=PACK)
         out_words = out_1[0].rearrange("p c r -> p (c r)").bitcast(I32)
-        ys = [keep.tile([P, PACK * CHUNK], F32, name="y%d" % c) for c in range(CHUNKS)]
-        y_planes = [y[:].rearrange("p (t j) -> p t j", t=PACK) for y in ys]
+        y_all = keep.tile([P, CHUNKS * PACK * CHUNK], F32, name="y_all", tag="hid1", align_bytes=64)
+        y_planes = [
+            y_all[:, c * PACK * CHUNK : (c + 1) * PACK * CHUNK].rearrange("p (t j) -> p t j", t=PACK)
+            for c in range(CHUNKS)
+        ]
         y_bf = [keep.tile([P, PACK * CHUNK], BF16, name="y_bf%d" % c, align_bytes=64) for c in range(CHUNKS)]
 
         spread = CHUNKS - TURNED
@@ -169,32 +170,8 @@ def tile_list_hidden_above_table_pl_kernel(
         for s in range(spread):
             c = TURNED + s
             nc.tensor.transpose(rw_bank[:, s * P : (s + 1) * P], rwc[:, c : c + 1].to_broadcast([P, P]), ident[:])
-        rw_rows = keep.tile([P, spread * CHUNK], F32, name="rw_rows")
+        rw_rows = keep.tile([P, spread * CHUNK], F32, name="rw_rows", tag="rw_rows", align_bytes=64)
         nc.scalar.copy(out=rw_rows[:], in_=rw_bank[:, : spread * P])
-
-        for c in range(TURNED):
-            cols = slice(c * CHUNK, (c + 1) * CHUNK)
-            p_t = bank(CHUNKS + c)
-            nc.tensor.matmul_mx(
-                out=p_t[:],
-                lhsT=hid_codes[c][:].bitcast(FP8X4),
-                lhsT_scale=hid_scales[c][:],
-                rhs=wbw[:].bitcast(FP4X4),
-                rhs_scale=wbs[:],
-                start=True,
-                stop=True,
-            )
-            y_rows = keep.tile([P, N], F32, name="y_rows%d" % c)
-            nc.scalar.activation(
-                out=y_rows[:].rearrange("p (t m) -> p t m", t=PACK),
-                in_=p_t[:].rearrange("p (m t) -> p t m", t=PACK),
-                func=COPY,
-                scale=rwc[:, c : c + 1],
-            )
-            y_bank = bank(c)
-            turn(y_rows, y_bank)
-            nc.scalar.copy(out=ys[c][:], in_=y_bank[:])
-            nc.sync.dma_start(out=out_rows[:, :, cols], in_=y_planes[c])
 
         for c in range(TURNED, CHUNKS):
             cols = slice(c * CHUNK, (c + 1) * CHUNK)
@@ -228,10 +205,9 @@ def tile_list_hidden_above_table_pl_kernel(
                 )
             nc.sync.dma_start(out=out_rows[:, :, cols], in_=y_planes[c])
 
+        y_codes = keep.tile([P, J], U32, name="y_codes", tag="rw_rows", align_bytes=64)
         for c in range(CHUNKS):
             cols = slice(c * CHUNK, (c + 1) * CHUNK)
-            if c < TURNED:
-                nc.vector.tensor_copy(out=woven(y_bf[c][:]), in_=by_lines(y_planes[c]))
             nc.vector.quantize_mx(out=y_codes[:, cols].bitcast(FP8X4), scales=y_scales[:, cols], in_=y_bf[c][:])
             if c == CHUNKS - 2:
                 nc.sync.dma_start(out=out_words[:, : (c + 1) * CHUNK], in_=y_codes[:, : (c + 1) * CHUNK].bitcast(I32))

@@ -27,8 +27,8 @@ MULT = mybir.AluOpType.mult
 
 
 def load_scales(queue, plane, rows):
-    for q in range(4):
-        queue.dma_start(out=plane[32 * q : 32 * q + 4, :].bitcast(I32), in_=rows[4 * q : 4 * q + 4, :].bitcast(I32))
+    for r in range(4):
+        queue.dma_start(out=plane[r:P:32, :].bitcast(I32), in_=rows[r:16:4, :].bitcast(I32))
 
 
 def by_lines(planes):
@@ -56,7 +56,7 @@ def tile_list_hidden_above_table_pl_kernel(
         xs = keep.tile([P, T], U8, name="xs", align_bytes=64)
         waw = keep.tile([P, R], U32, name="waw", align_bytes=64)
         was = keep.tile([P, R], U8, name="was", align_bytes=64)
-        wbw = keep.tile([P, N], U16, name="wbw", tag="hid0", align_bytes=64)
+        wbw = keep.tile([P, N], U16, name="wbw", align_bytes=64)
         wbs = keep.tile([P, N], U8, name="wbs", tag="hid1", align_bytes=64)
         rwc = keep.tile([P, CHUNKS], F32, name="rwc")
         ident = keep.tile([P, P], F32, name="ident")
@@ -155,14 +155,12 @@ def tile_list_hidden_above_table_pl_kernel(
             hid_codes.append(codes)
             hid_scales.append(scales)
 
+        y_codes = keep.tile([P, J], U32, name="y_codes", align_bytes=64)
         y_scales = keep.tile([P, J], U8, name="y_scales", align_bytes=64)
         out_rows = out_0.rearrange("(p t) j -> p t j", t=PACK)
         out_words = out_1[0].rearrange("p c r -> p (c r)").bitcast(I32)
-        y_all = keep.tile([P, CHUNKS * PACK * CHUNK], F32, name="y_all", tag="hid1", align_bytes=64)
-        y_planes = [
-            y_all[:, c * PACK * CHUNK : (c + 1) * PACK * CHUNK].rearrange("p (t j) -> p t j", t=PACK)
-            for c in range(CHUNKS)
-        ]
+        ys = [keep.tile([P, PACK * CHUNK], F32, name="y%d" % c) for c in range(CHUNKS)]
+        y_planes = [y[:].rearrange("p (t j) -> p t j", t=PACK) for y in ys]
         y_bf = [keep.tile([P, PACK * CHUNK], BF16, name="y_bf%d" % c, align_bytes=64) for c in range(CHUNKS)]
 
         spread = CHUNKS - TURNED
@@ -170,7 +168,7 @@ def tile_list_hidden_above_table_pl_kernel(
         for s in range(spread):
             c = TURNED + s
             nc.tensor.transpose(rw_bank[:, s * P : (s + 1) * P], rwc[:, c : c + 1].to_broadcast([P, P]), ident[:])
-        rw_rows = keep.tile([P, spread * CHUNK], F32, name="rw_rows", tag="rw_rows", align_bytes=64)
+        rw_rows = keep.tile([P, spread * CHUNK], F32, name="rw_rows")
         nc.scalar.copy(out=rw_rows[:], in_=rw_bank[:, : spread * P])
 
         for c in range(TURNED, CHUNKS):
@@ -205,13 +203,12 @@ def tile_list_hidden_above_table_pl_kernel(
                 )
             nc.sync.dma_start(out=out_rows[:, :, cols], in_=y_planes[c])
 
-        y_codes = keep.tile([P, J], U32, name="y_codes", tag="rw_rows", align_bytes=64)
         for c in range(CHUNKS):
             cols = slice(c * CHUNK, (c + 1) * CHUNK)
             nc.vector.quantize_mx(out=y_codes[:, cols].bitcast(FP8X4), scales=y_scales[:, cols], in_=y_bf[c][:])
-            if c == CHUNKS - 2:
-                nc.sync.dma_start(out=out_words[:, : (c + 1) * CHUNK], in_=y_codes[:, : (c + 1) * CHUNK].bitcast(I32))
-        nc.sync.dma_start(out=out_words[:, last * CHUNK :], in_=y_codes[:, last * CHUNK :].bitcast(I32))
+            if c % 2:
+                done = slice((c - 1) * CHUNK, (c + 1) * CHUNK)
+                nc.sync.dma_start(out=out_words[:, done], in_=y_codes[:, done].bitcast(I32))
         for q in range(4):
             queue = nc.scalar if q % 2 else nc.sync
             queue.dma_start(

from contextlib import ExitStack

import concourse.mybir as mybir
from concourse.masks import make_identity

K, T, J, R, V, N = 512, 2048, 512, 512, 1024, 512
FLOPS = 2 * K * R * J + 2 * R * N * J

F32 = mybir.dt.float32
BF16 = mybir.dt.bfloat16
I32 = mybir.dt.int32
U32 = mybir.dt.uint32
U16 = mybir.dt.uint16
U8 = mybir.dt.uint8
FP8X4 = mybir.dt.float8_e4m3fn_x4
FP4X4 = mybir.dt.float4_e2m1fn_x4
COPY = mybir.ActivationFunctionType.Copy
MAX = mybir.AluOpType.max

P = 128
PACK = 4
CHUNK = 128
CHUNKS = J // CHUNK
LIST_COLS = CHUNK // 16
TURNED = 0
MULT = mybir.AluOpType.mult


def load_scales(queue, plane, rows):
    for r in range(4):
        queue.dma_start(out=plane[r:P:32, :].bitcast(I32), in_=rows[r:16:4, :].bitcast(I32))


def by_lines(planes):
    return planes.rearrange("p t (c i) -> p c t i", i=PACK)


def woven(tile):
    return tile.rearrange("p (c i t) -> p c t i", i=PACK, t=PACK)


def tile_list_hidden_above_table_pl_kernel(
    tc, xt_words, xt_scales, wa_words, wa_scales, tb, wb_words, wb_scales, rw, offs, offs2, out_0, out_1, out_2
):
    nc = tc.nc
    with ExitStack() as ctx:
        keep = ctx.enter_context(tc.tile_pool(name="keep", bufs=1))
        psum = ctx.enter_context(tc.psum_pool(name="psum", bufs=1))

        def bank(b):
            return psum.tile([P, 512], F32, name="bank%d" % b, tag="bank%d" % b)

        idx = keep.tile([P, J // 16], U16, name="idx")
        idx2 = keep.tile([P, J // 16], U16, name="idx2")
        xw = keep.tile([P, T], U16, name="xw", align_bytes=64)
        xs = keep.tile([P, T], U8, name="xs", align_bytes=64)
        waw = keep.tile([P, R], U32, name="waw", align_bytes=64)
        was = keep.tile([P, R], U8, name="was", align_bytes=64)
        wbw = keep.tile([P, N], U16, name="wbw", align_bytes=64)
        wbs = keep.tile([P, N], U8, name="wbs", tag="hid1", align_bytes=64)
        rwc = keep.tile([P, CHUNKS], F32, name="rwc")
        ident = keep.tile([P, P], F32, name="ident")
        table = [keep.tile([P, V], F32, name="table%d" % t) for t in range(PACK)]

        nc.vector.memset(xs[:].bitcast(I32), 0)
        nc.gpsimd.memset(was[:].bitcast(I32), 0)
        nc.vector.memset(wbs[:].bitcast(I32), 0)
        make_identity(nc, ident[:])

        tb_rows = tb.rearrange("(p t) v -> p t v", t=PACK)
        nc.sync.dma_start(idx[:], offs)
        nc.sync.dma_start(out=xw[:].bitcast(I32), in_=xt_words[0].bitcast(I32))
        load_scales(nc.sync, xs, xt_scales[0])
        nc.sync.dma_start(out=waw[:].bitcast(I32), in_=wa_words[0].rearrange("p c r -> p (c r)").bitcast(I32))
        nc.sync.dma_start(idx2[:], offs2)
        for t in range(PACK):
            nc.sync.dma_start(out=table[t][:], in_=tb_rows[:, t, :])
            if t == 1:
                load_scales(nc.sync, was, wa_scales[0])
        nc.sync.dma_start(out=wbw[:].bitcast(I32), in_=wb_words[0].bitcast(I32))
        load_scales(nc.sync, wbs, wb_scales[0])
        with nc.allow_non_contiguous_dma(reason="one slot weight a partition and chunk"):
            nc.sync.dma_start(out=rwc[:], in_=rw[0].rearrange("(c p) -> p c", p=P))

        xg = keep.tile([P, J], U16, name="xg", align_bytes=64)
        xsg = keep.tile([P, J], U8, name="xsg", align_bytes=64)
        floor = keep.tile([P, PACK * J], F32, name="floor")
        floor_planes = floor[:].rearrange("p (t j) -> p t j", t=PACK)

        nc.vector.tensor_copy(xg[:], xw[:].indirect(idx[:]))
        nc.vector.tensor_copy(xsg[:], xs[:].indirect(idx[:]))
        for t in range(PACK - 1):
            nc.vector.tensor_copy(floor[:, t * J : (t + 1) * J], table[t][:].indirect(idx2[:]))

        def turn(rows, dst):
            for t in range(PACK):
                nc.tensor.transpose(dst[:, t * P : (t + 1) * P], rows[:, t * P : (t + 1) * P], ident[:])

        a_banks = []
        for c in range(CHUNKS):
            cols = slice(c * CHUNK, (c + 1) * CHUNK)
            a_t = bank(CHUNKS + c)
            nc.tensor.matmul_mx(
                out=a_t[:],
                lhsT=xg[:, cols].bitcast(FP4X4),
                lhsT_scale=xsg[:, cols],
                rhs=waw[:].bitcast(FP8X4),
                rhs_scale=was[:],
                start=True,
                stop=True,
            )
            a_rows = keep.tile([P, R], F32, name="a_rows%d" % c)
            nc.scalar.copy(
                out=a_rows[:].rearrange("p (t m) -> p t m", t=PACK),
                in_=a_t[:].rearrange("p (m t) -> p t m", t=PACK),
            )
            a_bank = bank(c)
            turn(a_rows, a_bank)
            a_banks.append(a_bank)

        wbw_dealt = keep.tile([P, N], U16, name="wbw_dealt", align_bytes=64)
        wbs_dealt = keep.tile([P, N], U8, name="wbs_dealt", align_bytes=64)
        last = PACK - 1
        nc.vector.tensor_copy(
            out=wbw_dealt[:].rearrange("p (t c i) -> p c t i", t=PACK, i=8),
            in_=wbw[:].rearrange("p (c i t) -> p c t i", t=PACK, i=8),
        )
        nc.vector.tensor_copy(
            out=wbs_dealt[:].rearrange("p (t c i) -> p c t i", t=PACK, i=16),
            in_=wbs[:].rearrange("p (c i t) -> p c t i", t=PACK, i=16),
        )
        hid_codes = []
        hid_scales = []
        for c in range(CHUNKS):
            cols = slice(c * CHUNK, (c + 1) * CHUNK)
            nc.vector.tensor_copy(
                floor[:, last * J + c * CHUNK : last * J + (c + 1) * CHUNK],
                table[last][:].indirect(idx2[:, c * LIST_COLS : (c + 1) * LIST_COLS]),
            )
            if c < 1:
                hid = keep.tile([P, PACK * CHUNK], BF16, name="hid%d" % c, tag="hid%d" % c, align_bytes=64)[:]
            else:
                if c == 1:
                    hid_late = keep.tile([P, 3 * PACK * CHUNK], BF16, name="hid_late", tag="hid1", align_bytes=64)
                hid = hid_late[:, (c - 1) * PACK * CHUNK : c * PACK * CHUNK]
            nc.vector.tensor_tensor(
                out=woven(hid),
                in0=by_lines(a_banks[c][:].rearrange("p (t j) -> p t j", t=PACK)),
                in1=by_lines(floor_planes[:, :, cols]),
                op=MAX,
            )
            codes = keep.tile([P, CHUNK], U32, name="hid_codes%d" % c, align_bytes=64)
            scales = keep.tile([P, CHUNK], U8, name="hid_scales%d" % c, align_bytes=64)
            nc.vector.quantize_mx(out=codes[:].bitcast(FP8X4), scales=scales[:], in_=hid)
            hid_codes.append(codes)
            hid_scales.append(scales)

        y_codes = keep.tile([P, J], U32, name="y_codes", align_bytes=64)
        y_scales = keep.tile([P, J], U8, name="y_scales", align_bytes=64)
        out_rows = out_0.rearrange("(p t) j -> p t j", t=PACK)
        out_words = out_1[0].rearrange("p c r -> p (c r)").bitcast(I32)
        ys = [keep.tile([P, PACK * CHUNK], F32, name="y%d" % c) for c in range(CHUNKS)]
        y_planes = [y[:].rearrange("p (t j) -> p t j", t=PACK) for y in ys]
        y_bf = [keep.tile([P, PACK * CHUNK], BF16, name="y_bf%d" % c, align_bytes=64) for c in range(CHUNKS)]

        spread = CHUNKS - TURNED
        rw_bank = bank(2 * CHUNKS - 1)
        for s in range(spread):
            c = TURNED + s
            nc.tensor.transpose(rw_bank[:, s * P : (s + 1) * P], rwc[:, c : c + 1].to_broadcast([P, P]), ident[:])
        rw_rows = keep.tile([P, spread * CHUNK], F32, name="rw_rows")
        nc.scalar.copy(out=rw_rows[:], in_=rw_bank[:, : spread * P])

        for c in range(TURNED, CHUNKS):
            cols = slice(c * CHUNK, (c + 1) * CHUNK)
            p_bank = bank(CHUNKS + c)
            for t in range(PACK):
                nc.tensor.matmul_mx(
                    out=p_bank[:, t * CHUNK : (t + 1) * CHUNK],
                    lhsT=wbw_dealt[:, t * P : (t + 1) * P].bitcast(FP4X4),
                    lhsT_scale=wbs_dealt[:, t * P : (t + 1) * P],
                    rhs=hid_codes[c][:].bitcast(FP8X4),
                    rhs_scale=hid_scales[c][:],
                    start=True,
                    stop=True,
                )
            s = c - TURNED
            parts = 2 if c == CHUNKS - 1 else 1
            width = CHUNK // parts
            for h in range(parts):
                part = slice(h * width, (h + 1) * width)
                nc.vector.tensor_tensor(
                    out=y_planes[c][:, :, part],
                    in0=p_bank[:].rearrange("p (t j) -> p t j", t=PACK)[:, :, part],
                    in1=rw_rows[:, s * CHUNK + h * width : s * CHUNK + (h + 1) * width]
                    .unsqueeze(1)
                    .to_broadcast([P, PACK, width]),
                    op=MULT,
                )
                nc.scalar.copy(
                    out=woven(y_bf[c][:, PACK * h * width : PACK * (h + 1) * width]),
                    in_=by_lines(y_planes[c][:, :, part]),
                )
            nc.sync.dma_start(out=out_rows[:, :, cols], in_=y_planes[c])

        for c in range(CHUNKS):
            cols = slice(c * CHUNK, (c + 1) * CHUNK)
            nc.vector.quantize_mx(out=y_codes[:, cols].bitcast(FP8X4), scales=y_scales[:, cols], in_=y_bf[c][:])
            if c % 2:
                done = slice((c - 1) * CHUNK, (c + 1) * CHUNK)
                nc.sync.dma_start(out=out_words[:, done], in_=y_codes[:, done].bitcast(I32))
        for q in range(4):
            queue = nc.scalar if q % 2 else nc.sync
            queue.dma_start(
                out=out_2[0, 4 * q : 4 * q + 4, :].bitcast(I32), in_=y_scales[32 * q : 32 * q + 4, :].bitcast(I32)
            )
